import numpy as np
import ml_dtypes


def mxq(x, axis, fmt="e4m3"):
    dtype, down = {"e4m3": (ml_dtypes.float8_e4m3fn, 7), "e5m2": (ml_dtypes.float8_e5m2, 14)}[fmt]
    v = np.moveaxis(np.asarray(x, np.float32).astype(ml_dtypes.bfloat16).astype(np.float64), axis, -1)
    blocks = v.reshape(v.shape[:-1] + (-1, 32))
    amax = np.abs(blocks).max(-1, keepdims=True)
    byte = np.maximum(np.where(amax > 0, np.frexp(amax)[1] - 1 + 127, 0) - down, 1)
    scale = np.exp2(byte - 127.0)
    codes = (blocks / scale).astype(np.float32).astype(dtype).astype(np.float64)
    return np.moveaxis((codes * scale).reshape(v.shape), -1, axis)


WIDE = False


def mx_kscale(k):
    if not WIDE:
        return np.ones(k)
    levels = np.array([10, -10, 5, -5, 0])
    if k % 512:
        return np.exp2(np.random.permutation(np.resize(levels, k // 32))).repeat(32)
    a = np.empty((k // 512, 16))
    for p in range(k // 512):
        a[p, :8] = np.random.permutation(np.resize(levels, 8))
        for g in range(8):
            far = levels[np.abs(levels - a[p, g]) >= 10]
            a[p, g + 8] = far[np.random.randint(len(far))]
    return np.exp2(a.ravel()).repeat(32)


BF16 = ml_dtypes.bfloat16


def bf(x):
    return np.asarray(x, np.float32).astype(BF16)


def f64(x):
    return np.asarray(x).astype(np.float64)


E2M1 = np.array([0.0, 0.5, 1.0, 1.5, 2.0, 3.0, 4.0, 6.0, -0.0, -0.5, -1.0, -1.5, -2.0, -3.0, -4.0, -6.0])


def pack_weight(w, fmt):
    k, n = w.shape
    w = f64(bf(w)).reshape(k // 32, 32, n)
    amax = np.abs(w).max(1)
    if fmt == "e4m3":
        byte = np.frexp(amax)[1] - 1 + 127 - 7
    else:
        mant, ex = np.frexp(amax / 6.0)
        byte = np.where(mant > 0.5, ex, ex - 1) + 127
    byte = np.clip(np.where(amax > 0, byte, 1), 1, 254)
    scaled = (w * np.exp2(127.0 - byte)[:, None, :]).reshape(k, n).astype(np.float32)
    by_word = np.ascontiguousarray(scaled.reshape(k // 512, 128, 4, n).transpose(0, 1, 3, 2))
    if fmt == "e4m3":
        words = by_word.astype(ml_dtypes.float8_e4m3fn).view(np.uint8)
    else:
        c = by_word.astype(ml_dtypes.float4_e2m1fn).view(np.uint8) & 0xF
        words = c[..., 0::2] | (c[..., 1::2] << 4)
    return np.ascontiguousarray(words), np.ascontiguousarray(byte.astype(np.uint8).reshape(k // 512, 16, n))


def unpack_weight(words, scales, fmt):
    g, p, n, _ = words.shape
    if fmt == "e4m3":
        vals = np.ascontiguousarray(words).view(ml_dtypes.float8_e4m3fn).astype(np.float64)
    else:
        nib = np.empty((g, p, n, 4), np.uint8)
        nib[..., 0::2] = words & 0xF
        nib[..., 1::2] = words >> 4
        vals = E2M1[nib]
    vals = vals * np.repeat(np.exp2(scales.astype(np.float64) - 127.0), 8, axis=1)[..., None]
    return vals.transpose(0, 1, 3, 2).reshape(g * 512, n)
def pack4(w):
    words, scales = pack_weight(w, "e2m1")
    return words.reshape(words.shape[0], 128, -1), scales


def unpack4(words, scales):
    return unpack_weight(words.reshape(words.shape[0], 128, -1, 2), scales, "e2m1")


T, D, A, M = 1024, 2048, 1024, 1024


def setup_inputs():
    s, c = mx_kscale(D), mx_kscale(A)
    b_words, b_scales = pack4(np.random.standard_normal((A, M)) / np.sqrt(A) / c[:, None])
    return {"x": bf(np.random.standard_normal((T, D)) * s),
            "phi": bf(np.random.standard_normal((D, M)) / np.sqrt(D) / s[:, None]),
            "u": bf(np.random.standard_normal((T, A)) * c),
            "b_words": b_words,
            "b_scales": b_scales,
            "rate": bf(np.random.standard_normal((T, M))),
            "damp": bf(0.6 * (1 + 0.1 * np.random.standard_normal(M))),
            "step": bf(0.5 * (1 + 0.1 * np.random.standard_normal(T)))}


def reference(x, phi, u, b_words, b_scales, rate, damp, step):
    restoring = mxq(f64(x), 1, "e4m3") @ mxq(f64(phi), 0, "e4m3")
    control = mxq(f64(u), 1, "e4m3") @ unpack4(b_words, b_scales)
    force = restoring + control
    r = f64(rate)
    acc = force - f64(damp) * r
    rate_next = r + f64(step)[:, None] * acc
    return acc, rate_next

from contextlib import ExitStack

import concourse.mybir as mybir
from concourse.masks import make_identity

T, D, A, M = 1024, 2048, 1024, 1024
FLOPS = 2 * T * (D + A) * M

F32 = mybir.dt.float32
BF16 = mybir.dt.bfloat16
I32 = mybir.dt.int32
U32 = mybir.dt.uint32
U8 = mybir.dt.uint8
FP8X4 = mybir.dt.float8_e4m3fn_x4
FP4X4 = mybir.dt.float4_e2m1fn_x4
ALU = mybir.AluOpType

P = 128
PACK = 4
K_PASS = P * PACK
N_HALF = 512
TILES = T // P
X_PASSES = D // K_PASS
U_PASSES = A // K_PASS
TURN_BANKS = (4, 5, 6, 7)
GROUPED_BUFS = 4
WOVEN_BUFS = 3
DAMPED_BUFS = 4
OUT_BUFS = 9
FIRST = 3
AHEAD = 2
HEAD = 2
V_COLS = 320


def tile_modal_vibration_step_s1_kernel(tc, x, phi, u, b_words, b_scales, rate, damp, step, out_0, out_1):
    nc = tc.nc
    x_t = x.rearrange("(p i) k -> p i k", i=TILES)
    u_t = u.rearrange("(p i) k -> p i k", i=TILES)
    rate_t = rate.rearrange("(p i) m -> p i m", i=TILES)
    acc_t = out_0.rearrange("(p i) m -> p i m", i=TILES)
    next_t = out_1.rearrange("(p i) m -> p i m", i=TILES)
    b_words32 = b_words.bitcast(I32)
    b_scales32 = b_scales.bitcast(I32)

    with ExitStack() as ctx:
        keep = ctx.enter_context(tc.tile_pool(name="keep", bufs=1))
        ring = ctx.enter_context(tc.tile_pool(name="ring", bufs=1))
        psum = ctx.enter_context(tc.psum_pool(name="psum", bufs=1))
        ctx.enter_context(tc.manual_schedule())

        ident = keep.tile([P, P], F32, name="ident")
        make_identity(nc, ident[:])
        b_plane = keep.tile([P, U_PASSES, M], U8, name="b_plane", align_bytes=64)
        damp_rows = keep.tile([P, M // P], BF16, name="damp_rows")
        damp_all = keep.tile([P, M], BF16, name="damp_all")
        step_sb = keep.tile([P, TILES], BF16, name="step_sb")

        raw, rate_sb, b_sb, phi_raw = {}, {}, {}, {}
        grouped, codes, scales = {}, {}, {}
        woven, phi_codes, phi_scales = {}, {}, {}
        sums, damped_sb, acc_sb, next_sb = {}, {}, {}, {}
        turns = []

        def cols(h):
            return slice(h * N_HALF, (h + 1) * N_HALF)

        def bank(b):
            return psum.tile([P, N_HALF], F32, name="bank%d" % b)

        def load_small():
            nc.scalar.dma_start(out=damp_rows[:], in_=damp.rearrange("(p c) -> p c", p=P))
            nc.scalar.dma_start(out=step_sb[:], in_=step.rearrange("(p i) -> p i", p=P))
            plane32 = b_plane[:].rearrange("p g n -> p (g n)").bitcast(I32)
            nc.vector.memset(plane32, 0)
            for q in range(4):
                nc.scalar.dma_start(
                    out=plane32[32 * q : 32 * q + 4, :].rearrange("r (g n) -> r g n", g=U_PASSES),
                    in_=b_scales32[:, 4 * q : 4 * q + 4, :].rearrange("g r n -> r g n"),
                )

        def load_u(i):
            raw[i, "u"] = keep.tile([P, A], BF16, name="u%d" % i)
            nc.sync.dma_start(out=raw[i, "u"][:], in_=u_t[:, i, :])

        def load_x(i):
            raw[i, "x"] = keep.tile([P, D], BF16, name="x%d" % i)
            nc.sync.dma_start(out=raw[i, "x"][:], in_=x_t[:, i, :])

        def load_b(h):
            b_sb[h] = keep.tile([P, U_PASSES * 2 * N_HALF], U8, name="b%d" % h, align_bytes=64)
            words = N_HALF // 2
            nc.sync.dma_start(
                out=b_sb[h][:].bitcast(I32).rearrange("p (g n) -> p g n", g=U_PASSES),
                in_=b_words32[:, :, h * words : (h + 1) * words].rearrange("g p n -> p g n"),
            )

        def load_phi(g, h):
            phi_raw[g, h] = keep.tile([P, PACK, N_HALF], BF16, name="phi%d_%d" % (g, h))
            rows = phi[g * K_PASS : (g + 1) * K_PASS, cols(h)]
            nc.sync.dma_start(out=phi_raw[g, h][:], in_=rows.rearrange("(p j) n -> p j n", j=PACK))

        def load_rate(i0, n, h):
            some = keep.tile([P, n, N_HALF], BF16, name="rate%d_%d" % (i0, h))
            nc.sync.dma_start(out=some[:], in_=rate_t[:, i0 : i0 + n, cols(h)])
            for i in range(n):
                rate_sb[i0 + i, h] = some[:, i, :]

        def spread_damp():
            words = damp_rows[:].bitcast(F32)
            into = bank(TURN_BANKS[-1])
            for c in range(4):
                nc.tensor.transpose(into[:, c * P : (c + 1) * P], words[:, c : c + 1].to_broadcast([P, P]), ident[:])
            nc.scalar.copy(
                out=damp_all[:].bitcast(F32).rearrange("p (n c) -> p n c", c=4),
                in_=into[:].rearrange("p (c n) -> p n c", c=4),
            )

        def turn(i, c):
            words = raw[i, "u" if c == 0 else "x"][:].bitcast(F32)
            first = 0 if c == 0 else (c - 1) * 512
            into = bank(TURN_BANKS[len(turns) % len(TURN_BANKS)])
            turns.append((i, c))
            for g in range(2):
                for e in range(2):
                    at = first + 256 * g
                    slot = 2 * g + e
                    nc.tensor.transpose(into[:, slot * P : (slot + 1) * P], words[:, at + e : at + 256 : 2], ident[:])
            grouped[i, c] = ring.tile([P, 2 * K_PASS], BF16, name="grouped", bufs=GROUPED_BUFS, align_bytes=64)
            nc.scalar.copy(
                out=grouped[i, c][:].bitcast(F32).rearrange("p (g r e) -> p g r e", g=2, e=2),
                in_=into[:].rearrange("p (g e r) -> p g r e", g=2, e=2),
            )

        def quant(i, c):
            codes[i, c] = keep.tile([P, 2 * P], U32, name="codes%d_%d" % (i, c), align_bytes=64)
            scales[i, c] = keep.tile([P, 2 * P], U8, name="scales%d_%d" % (i, c), align_bytes=64)
            nc.vector.quantize_mx(out=codes[i, c][:].bitcast(FP8X4), scales=scales[i, c][:], in_=grouped[i, c][:])

        def weave(engine, g, h, c0, c1):
            if (g, h) not in woven:
                woven[g, h] = ring.tile([P, N_HALF, PACK], BF16, name="woven", bufs=WOVEN_BUFS, align_bytes=64)
            dst = woven[g, h][:, c0:c1, :].rearrange("p (c i) t -> p c t i", i=4)
            src = phi_raw[g, h][:, :, c0:c1].rearrange("p t (c i) -> p c t i", i=4)
            if engine == "vector":
                nc.vector.tensor_copy(out=dst, in_=src)
            else:
                nc.scalar.copy(out=dst, in_=src)

        def quant_phi(g, h):
            phi_codes[g, h] = keep.tile([P, N_HALF], U32, name="phi_codes%d_%d" % (g, h), align_bytes=64)
            phi_scales[g, h] = keep.tile([P, N_HALF], U8, name="phi_scales%d_%d" % (g, h), align_bytes=64)
            nc.vector.quantize_mx(
                out=phi_codes[g, h][:].bitcast(FP8X4),
                scales=phi_scales[g, h][:],
                in_=woven[g, h][:].rearrange("p n t -> p (n t)"),
            )

        def mm_u(i, h):
            sums[i, h] = bank(i % 4 if h == 0 else (i + 4) % 8)
            for g in range(U_PASSES):
                nc.tensor.matmul_mx(
                    out=sums[i, h][:],
                    lhsT=codes[i, 0][:, g * P : (g + 1) * P].bitcast(FP8X4),
                    lhsT_scale=scales[i, 0][:, g * P : (g + 1) * P],
                    rhs=b_sb[h][:, g * 2 * N_HALF : (g + 1) * 2 * N_HALF].bitcast(FP4X4),
                    rhs_scale=b_plane[:, g, cols(h)],
                    start=(g == 0),
                    stop=False,
                )

        def mm_x(i, g, h):
            c, at = 1 + g // 2, (g % 2) * P
            nc.tensor.matmul_mx(
                out=sums[i, h][:],
                lhsT=codes[i, c][:, at : at + P].bitcast(FP8X4),
                lhsT_scale=scales[i, c][:, at : at + P],
                rhs=phi_codes[g, h][:].bitcast(FP8X4),
                rhs_scale=phi_scales[g, h][:],
                start=False,
                stop=(g == X_PASSES - 1),
            )

        def damped(i, h):
            damped_sb[i, h] = ring.tile([P, N_HALF], F32, name="damped", bufs=DAMPED_BUFS)
            nc.vector.tensor_tensor(out=damped_sb[i, h][:], in0=rate_sb[i, h], in1=damp_all[:, cols(h)], op=ALU.mult)

        def accel(i, h):
            acc_sb[i, h] = ring.tile([P, N_HALF], F32, name="acc", bufs=OUT_BUFS)
            nc.vector.tensor_tensor(out=acc_sb[i, h][:], in0=sums[i, h][:], in1=damped_sb[i, h][:], op=ALU.subtract)

        def advance(i, h):
            next_sb[i, h] = ring.tile([P, N_HALF], F32, name="next", bufs=OUT_BUFS)
            nc.vector.scalar_tensor_tensor(
                out=next_sb[i, h][:], in0=acc_sb[i, h][:], scalar=step_sb[:, i : i + 1], in1=rate_sb[i, h],
                op0=ALU.mult, op1=ALU.add,
            )

        def store(i, h):
            nc.sync.dma_start(out=acc_t[:, i, cols(h)], in_=acc_sb[i, h][:])
            nc.sync.dma_start(out=next_t[:, i, cols(h)], in_=next_sb[i, h][:])

        load_small()
        load_u(0); load_b(0); load_x(0); load_phi(0, 0)
        load_u(1); load_x(1); load_phi(1, 0); load_phi(2, 0)
        load_u(2); load_x(2); load_phi(3, 0)
        load_rate(0, 2, 0); load_u(3); load_x(3); load_phi(0, 1)
        load_u(4); load_x(4); load_rate(2, 2, 0)
        load_u(5); load_x(5); load_phi(1, 1); load_rate(4, 2, 0)
        load_u(6); load_x(6); load_phi(2, 1)
        load_u(7); load_x(7); load_phi(3, 1); load_rate(6, 2, 0); load_b(1)
        load_rate(0, 4, 1); load_rate(4, 4, 1)

        def weave_both(g):
            weave("vector", g, 0, 0, V_COLS)
            weave("scalar", g, 0, V_COLS, N_HALF)

        def mm_all(i, h):
            mm_u(i, h)
            for g in range(X_PASSES):
                mm_x(i, g, h)

        spread_damp()
        turn(0, 0); quant(0, 0); turn(0, 1); turn(0, 2); weave_both(0); quant(0, 1); quant(0, 2); mm_u(0, 0); quant_phi(0, 0)
        turn(1, 0); quant(1, 0); turn(1, 1); turn(1, 2); weave_both(1); quant(1, 1); quant(1, 2); mm_u(1, 0)
        mm_x(0, 0, 0); mm_x(1, 0, 0)
        weave_both(2); quant_phi(1, 0); quant_phi(2, 0)
        turn(2, 0); quant(2, 0); turn(2, 1); turn(2, 2); weave_both(3); quant(2, 1); quant(2, 2)
        mm_x(0, 1, 0); mm_x(1, 1, 0); mm_u(2, 0); mm_x(0, 2, 0); mm_x(1, 2, 0); mm_x(2, 0, 0); mm_x(2, 1, 0); mm_x(2, 2, 0)
        damped(0, 0); quant_phi(3, 0); damped(1, 0)
        turn(3, 0); turn(3, 1); turn(3, 2)
        for i in range(FIRST):
            mm_x(i, 3, 0)
        weave("scalar", 0, 1, 0, 128); weave("scalar", 0, 1, 128, 256)
        quant(3, 0); quant(3, 1); accel(0, 0); quant(3, 2); accel(1, 0); advance(0, 0); damped(2, 0); advance(1, 0)
        pieces = [(g, c) for g in range(X_PASSES) for c in range(0, N_HALF, 128)]
        for i in range(FIRST + 1, TILES):
            j = i - 2
            turn(i, 0); turn(i, 1); turn(i, 2)
            for g, c in pieces[AHEAD + 3 * (j - 2) : AHEAD + 3 * (j - 1)]:
                weave("scalar", g, 1, c, c + 128)
            mm_all(i - 1, 0)
            accel(j, 0); damped(j + 1, 0); quant(i, 0); advance(j, 0); quant(i, 1)
            if j > 2:
                quant_phi(j - 3, 1)
            quant(i, 2)
        for g, c in pieces[AHEAD + 12 :]:
            weave("scalar", g, 1, c, c + 128)
        mm_all(TILES - 1, 0)
        for i in range(TILES - 2):
            store(i, 0)
        accel(6, 0); damped(7, 0); advance(6, 0); store(6, 0)
        for i in range(HEAD):
            mm_u(i, 1)
            for g in range(X_PASSES - 1):
                mm_x(i, g, 1)
        accel(7, 0); damped(0, 1); quant_phi(X_PASSES - 1, 1); advance(7, 0); store(7, 0)
        damped(1, 1)
        for i in range(TILES):
            if i < HEAD:
                mm_x(i, X_PASSES - 1, 1)
            else:
                mm_all(i, 1)
            accel(i, 1)
            if i + 2 < TILES:
                damped(i + 2, 1)
            advance(i, 1)
            store(i, 1)
